import numpy as np, ml_dtypes
CORES = [242,247,114,119]
N = 4
import mx_ref
NC, K = 128, 3
CNT = [[0,48,80,0],[56,0,0,72],[56,16,0,56],[16,64,48,0]]
OFF = [[sum(c[:e]) for e in range(N + 1)] for c in CNT]
BF = ml_dtypes.bfloat16
def setup_inputs(rng):
    def f(*shape):
        return mx_ref.flush((rng.standard_normal(shape, dtype=np.float32) * np.exp2(rng.integers(-2, 3, shape[:-1] + (1,)))).astype(BF))
    return {"x": f(N, 128, 4 * NC), "w": f(N, 128, 512)}
def setup_inputs_blocks(rng):
    d = setup_inputs(rng)
    for k in ("x", "w"): d[k] = mx_ref.spread(d[k], rng, 4)
    return d
def setup_inputs_wide(rng):
    d = setup_inputs(rng)
    for k in ("x", "w"): d[k] = mx_ref.flush((d[k].astype(np.float32) * np.exp2(rng.integers(-8, 9, (N, 1, 1))).astype(np.float32)).astype(BF))
    return d
def setup_inputs_zeros(rng):
    d = setup_inputs(rng); v = d["x"].reshape(N, 128, -1, 4).copy()
    v[np.broadcast_to((rng.random((N, 1, v.shape[2], 1)) < 0.33), v.shape)] = 0
    d["x"] = v.reshape(d["x"].shape)
    return d
def reference(x, w):
    y = np.zeros((N, 128, K * NC), np.float32)
    for e in range(N):
        t = np.concatenate([x[j][:, 4 * OFF[j][(e - k) % N]:4 * OFF[j][(e - k) % N + 1]] for k in range(K) for j in range(N)], axis=1)
        y[e] = mx_ref.matmul(mx_ref.quantize(w[e]), mx_ref.quantize(t))
    return {"y": y}

@@ -1,0 +1,202 @@
+from concourse.bass import DstId, RemoteDMATransfer
+from concourse.mybir import dt
+
+WIDE = 480
+SCRATCH = {
+    "xin": ("sbuf", [128, 512], "bfloat16"),
+    "win": ("sbuf", [128, 512], "bfloat16"),
+    "wq": ("sbuf", [128, 128], "float8_e4m3fn_x4"),
+    "ws": ("sbuf", [128, 128], "uint8"),
+    "lc": ("sbuf", [128, WIDE], "float8_e4m3fn_x4"),
+    "ls": ("sbuf", [128, WIDE], "uint8"),
+    "ysb": ("sbuf", [128, 384], "float32"),
+    "ps": ("psum", [128, 2048], "float32"),
+}
+SEMAPHORES = (["xl", "wl", "qx", "qw", "sent", "fw", "st0", "st1"]
+              + ["c%d" % j for j in range(4)] + ["s%d" % j for j in range(4)]
+              + ["mm%d" % k for k in range(4)] + ["cp%d" % k for k in range(6)])
+NC = 128
+
+
+def _plan(CNT):
+    off = [[sum(c[:e]) for e in range(5)] for c in CNT]
+
+    def run(j, a, b):
+        return off[j][a], off[j][b + 1]
+    al = (0, NC)
+    lay = {0: [(2, al), (3, run(3, 0, 0)), (1, al), (3, run(3, 2, 2))],
+           1: [(2, al), (3, run(3, 0, 1)), (0, al)],
+           2: [(0, al), (1, run(1, 0, 0)), (3, al)],
+           3: [(2, al), (1, run(1, 3, 3)), (0, al)]}
+    place = {}
+    for d in lay:
+        at = NC
+        place[d] = [(d, 0, NC, 0)]
+        for j, (a, b) in lay[d]:
+            place[d].append((j, a, b, at))
+            at += b - a
+
+    def col(d, j, c):
+        for jj, a, b, at in place[d]:
+            if jj == j and a <= c < b:
+                return at + c - a
+        raise ValueError("no place")
+
+    def t(kind, span, d):
+        return kind, span[0], span[1], d
+    sends = {
+        0: [[t("c", al, 2)],
+            [t("s", al, 2), t("s", al, 3), t("s", al, 1)],
+            [t("c", run(0, 1, 1), 1)]],
+        1: [[t("c", run(1, 0, 0), 2), t("c", run(1, 0, 0), 0)],
+            [t("c", run(1, 3, 3), 3), t("c", run(1, 3, 3), 0)],
+            [t("s", run(1, 0, 0), 2), t("s", run(1, 0, 0), 0)],
+            [t("s", run(1, 3, 3), 3), t("s", run(1, 3, 3), 0)]],
+        2: [[t("c", al, 1)],
+            [t("s", al, 1), t("s", al, 3)],
+            [t("s", run(2, 0, 0), 0), t("s", run(2, 3, 3), 0)],
+            [t("c", run(2, 1, 3), 3)]],
+        3: [[t("c", run(3, 0, 1), 1)],
+            [t("c", run(3, 2, 2), 0)],
+            [t("s", run(3, 0, 1), 1), t("s", run(3, 0, 1), 2)],
+            [t("s", run(3, 2, 2), 0), t("s", run(3, 2, 2), 2)],
+            [t("s", run(3, 0, 0), 0)],
+            [t("c", al, 2)]]}
+    n0 = run(3, 0, 0)[1] - run(3, 0, 0)[0]
+    passes = {1: (["c2", "c3"], col(1, 2, 0), NC + n0, 0, col(0, 2, 0)),
+              2: (["c0"], col(2, 0, 0), NC, 3, col(3, 0, 0))}
+    q0 = col(0, 2, off[2][3])
+    p1 = col(0, 2, 0) + off[2][1]
+    windows = {
+        0: [(0, NC, [], [(0, 2)]),
+            (col(0, 1, 0), col(0, 3, off[3][2]) + CNT[3][2], ["c1", "s1", "c3", "s3"], [(1, 0), (1, 3), (3, 2)]),
+            (q0, q0 + NC, ["fw", "s2"], [(2, 3), (3, 0)]),
+            (p1 - NC, p1, [], [(2, 0)])],
+        1: [(0, NC, [], [(1, 0), (1, 3)]),
+            (col(1, 2, 0), col(1, 0, 0) + CNT[0][1], ["c0", "s0", "c2", "s2", "c3", "s3"],
+             [(2, 0), (3, 0), (2, 3), (0, 1), (2, 1), (3, 1)])],
+        2: [(0, NC, [], [(2, 1), (2, 0)]),
+            (col(2, 3, 0), col(2, 3, 0) + NC, ["c3", "s3"], [(3, 2), (3, 1), (3, 0)]),
+            (col(2, 0, 0), col(2, 1, 0) + CNT[1][0], ["c0", "s0", "c1", "s1"], [(0, 2), (0, 1), (1, 0)])],
+        3: [(0, NC, [], [(3, 1), (3, 2)]),
+            (col(3, 2, off[2][1]), col(3, 1, off[1][3]) + CNT[1][3], ["c2", "s2", "c1", "s1"], [(2, 1), (2, 3), (1, 3)]),
+            (col(3, 0, 0), col(3, 0, 0) + NC, ["fw", "s0"], [(0, 2), (0, 1)])]}
+
+    def ycol(e, j, f):
+        return NC * ((e - f) % 4) + sum(CNT[i][f] for i in range(j))
+
+    def yspan(e, j, f, j2, f2):
+        return ycol(e, j, f), ycol(e, j2, f2) + CNT[j2][f2]
+    stores = {
+        0: [(0, yspan(0, 1, 0, 1, 0)), (1, yspan(0, 1, 3, 1, 3)), (0, yspan(0, 0, 2, 3, 2)),
+            (1, yspan(0, 2, 3, 2, 3)), (0, yspan(0, 2, 0, 3, 0))],
+        1: [(0, yspan(1, 1, 0, 1, 0)), (1, yspan(1, 1, 3, 1, 3)),
+            (0, yspan(1, 2, 0, 3, 0)), (1, yspan(1, 2, 3, 2, 3)), (0, yspan(1, 0, 1, 3, 1))],
+        2: [(0, yspan(2, 3, 2, 3, 2)), (1, yspan(2, 2, 1, 3, 1)), (0, yspan(2, 2, 0, 3, 0)),
+            (1, yspan(2, 0, 2, 0, 2)), (0, yspan(2, 0, 1, 0, 1)), (1, yspan(2, 1, 0, 1, 0))],
+        3: [(0, yspan(3, 3, 2, 3, 2)), (1, yspan(3, 2, 1, 3, 1)), (0, yspan(3, 1, 3, 2, 3)),
+            (1, yspan(3, 0, 2, 0, 2)), (0, yspan(3, 0, 1, 0, 1))]}
+    return off, col, sends, passes, windows, ycol, stores
+
+
+def _bits(mask):
+    return [1 << k for k in range(mask.bit_length()) if mask >> k & 1]
+
+
+def _masks(call, src, cores, topo):
+    dsts = [cores[tr[3]] for tr in call]
+    away = [topo.host(d) != topo.host(src) or topo.chip(d) != topo.chip(src) for d in dsts]
+    far = [c for c in cores if topo.host(c) != topo.host(src)]
+    leave = topo.mask(src, far[0])
+    out = []
+    for k, d in enumerate(dsts):
+        pool = _bits(leave if away[k] else topo.mask(src, d) & ~leave)
+        share = len(pool) // away.count(away[k])
+        nth = away[:k].count(away[k])
+        out.append(sum(pool[nth * share:(nth + 1) * share]))
+    return out
+
+
+def rank_program(g, core, T, topo):
+    me = T.rank_of(core)
+    if me is None:
+        return
+    CNT = T.tables["CNT"]
+    cores = T.cores
+    off, col, sends, passes, windows, ycol, stores = _plan(CNT)
+
+    due = {}
+    sent = 0
+    for r in range(4):
+        for call in sends[r]:
+            for (kind, a, b, d), m in zip(call, _masks(call, cores[r], cores, topo)):
+                if d == me:
+                    due[kind + str(r)] = due.get(kind + str(r), 0) + m.bit_count()
+                if r == me:
+                    sent += m.bit_count()
+        if r in passes:
+            m = topo.mask(cores[r], cores[passes[r][3]])
+            if passes[r][3] == me:
+                due["fw"] = m.bit_count()
+            if r == me:
+                sent += m.bit_count()
+
+    g.sync.dma_start(T.xin[:], T.x[:]).then_inc(T.sem.xl, 16)
+    g.scalar.wait_ge(T.sem.xl, 16)
+    g.scalar.dma_start(T.win[:], T.w[:]).then_inc(T.sem.wl, 16)
+
+    g.vector.wait_ge(T.sem.xl, 16)
+    g.vector.quantize_mx(T.lc[:, 0:NC], T.ls[:, 0:NC], T.xin[:]).then_inc(T.sem.qx, 1)
+    g.vector.wait_ge(T.sem.wl, 16)
+    g.vector.quantize_mx(T.wq[:], T.ws[:], T.win[:]).then_inc(T.sem.qw, 1)
+
+    def side(kind, a, b):
+        return T.lc[:, a:b].bitcast(dt.uint8) if kind == "c" else T.ls[:, a:b]
+    g.wait_ge(T.sem.qx, 1)
+    for call in sends[me]:
+        trs = []
+        for (kind, a, b, d), m in zip(call, _masks(call, core, cores, topo)):
+            rid, pid = topo.addr(cores[d], core)
+            at = col(d, me, a)
+            trs.append((side(kind, at, at + b - a), side(kind, a, b), T.sem[kind + str(me)], rid, pid, m))
+        if len(trs) == 1:
+            o, i, s, rid, pid, m = trs[0]
+            g.remote_dma(out_ap=o, in_ap=i, remote_sem=s, local_sem=T.sem.sent, pid=pid, routing_id=rid, dma_engine_mask=m)
+        else:
+            g.remote_dma_fused([RemoteDMATransfer(dst_ids=[DstId(rid=rid, pnc=pid)], dma_engine_mask=m, remote_sem=s, src=i, dst=o)
+                                for o, i, s, rid, pid, m in trs], local_sem=T.sem.sent)
+    if me in passes:
+        waits, a, n, d, at = passes[me]
+        for s in waits:
+            g.wait_ge(T.sem[s], due[s])
+        rid, pid = topo.addr(cores[d], core)
+        g.remote_dma(out_ap=side("c", at, at + n), in_ap=side("c", a, a + n), remote_sem=T.sem.fw, local_sem=T.sem.sent,
+                     pid=pid, routing_id=rid, dma_engine_mask=topo.mask(core, cores[d]))
+    g.wait_ge(T.sem.sent, sent)
+
+    g.tensor.wait_ge(T.sem.qx, 1)
+    g.tensor.wait_ge(T.sem.qw, 1)
+    for k, (a, b, waits, runs) in enumerate(windows[me]):
+        for s in waits:
+            g.tensor.wait_ge(T.sem[s], due[s])
+        g.tensor.matmul_mx(T.ps[:, 512 * k:512 * k + b - a], T.wq[:], T.ws[:], T.lc[:, a:b], T.ls[:, a:b],
+                           True, True).then_inc(T.sem["mm%d" % k], 1)
+
+    ready = [0] * len(stores[me])
+    for k, (a, b, waits, runs) in enumerate(windows[me]):
+        g.vector.wait_ge(T.sem["mm%d" % k], 1)
+        for j, f in runs:
+            n, y = CNT[j][f], ycol(me, j, f)
+            p = 512 * k + col(me, j, off[j][f]) - a
+            s = [i for i, (q, (lo, hi)) in enumerate(stores[me]) if lo <= y and y + n <= hi][0]
+            ready[s] += 1
+            g.vector.tensor_copy(T.ysb[:, y:y + n], T.ps[:, p:p + n]).then_inc(T.sem["cp%d" % s], 1)
+
+    count = [0, 0]
+    for i, (q, (lo, hi)) in enumerate(stores[me]):
+        queue = g.scalar if q else g.sync
+        queue.wait_ge(T.sem["cp%d" % i], ready[i])
+        queue.dma_start(T.y[:, lo:hi], T.ysb[:, lo:hi]).then_inc(T.sem["st%d" % q], 16)
+        count[q] += 16
+    g.sync.wait_ge(T.sem.st0, count[0])
+    g.scalar.wait_ge(T.sem.st1, count[1])

@@ -1,7 +1,58 @@
 from concourse.bass import DstId, RemoteDMATransfer
 from concourse.mybir import dt
 
-WIDE = 480
+NC = 128
+WIDE = 512
+
+
+def _r(j, f0, f1):
+    return tuple((j, f) for f in range(f0, f1 + 1))
+
+
+LAY = {0: [(1, 0, 3), (2, 0, 3), (3, 0, 0), (0, 1, 2), (3, 2, 2)],
+       1: [(2, 0, 3), (3, 0, 1), (1, 0, 3), (0, 1, 2)],
+       2: [(1, 0, 0), (2, 0, 3), (0, 1, 2), (3, 0, 2)],
+       3: [(0, 1, 2), (3, 0, 2), (2, 1, 3), (1, 3, 3)]}
+CALLS = {
+    0: [([], [("c", _r(0, 2, 2), 3, "c0", "out")]),
+        ([], [("c", _r(0, 1, 1), 2, "c0", "out"), ("c", _r(0, 1, 1), 1, "c0", "in")]),
+        ([], [("s", _r(0, 1, 2), 2, "s0", "out"), ("s", _r(0, 1, 2), 3, "s0", "out"), ("s", _r(0, 1, 2), 1, "s0", "in")]),
+        (["c2"], [("c", _r(2, 0, 0), 1, "fw", "all")])],
+    1: [([], [("c", _r(1, 0, 0), 2, "c1", "out")]),
+        ([], [("c", _r(1, 0, 3), 0, "c1", "in")]),
+        ([], [("c", _r(1, 3, 3), 3, "c1", "out")]),
+        ([], [("s", _r(1, 0, 3), 0, "s1", "in")]),
+        ([], [("s", _r(1, 0, 0), 2, "s1", "out")]),
+        ([], [("s", _r(1, 3, 3), 3, "s1", "out")]),
+        (["c2", "c3"], [("c", _r(2, 1, 3) + _r(3, 0, 0), 0, "fw", "all")]),
+        (["s3"], [("s", _r(3, 0, 0), 0, "sf", "in")])],
+    2: [([], [("c", _r(2, 1, 3), 1, "c2", "out")]),
+        ([], [("c", _r(2, 0, 0), 0, "c2", "out")]),
+        ([], [("c", _r(2, 1, 3), 3, "c2", "in")]),
+        ([], [("s", _r(2, 0, 3), 1, "s2", "out"), ("s", _r(2, 0, 3), 0, "s2", "out")]),
+        ([], [("s", _r(2, 1, 3), 3, "s2", "in")]),
+        (["c0"], [("c", _r(0, 1, 1), 3, "fw", "all")])],
+    3: [([], [("c", _r(3, 0, 1), 1, "c3", "out")]),
+        ([], [("s", _r(3, 0, 1), 1, "s3", "out"), ("s", _r(3, 0, 1), 2, "s3", "in")]),
+        ([], [("c", _r(3, 2, 2), 0, "c3", "out")]),
+        ([], [("c", _r(3, 0, 2), 2, "c3", "in")]),
+        ([], [("s", _r(3, 2, 2), 0, "s3", "out"), ("s", _r(3, 2, 2), 2, "s3", "in")]),
+        (["c0"], [("c", _r(0, 2, 2), 2, "fw", "all")])]}
+WINDOWS = {
+    0: [(["c1", "s1"], [[(1, 0)], [(1, 3)]]), (["c3", "s3"], [[(0, 2), (3, 2)]]), (["c2", "s2"], [[(2, 0)]]),
+        (["fw"], [[(2, 3)]]), (["sf"], [[(3, 0)]])],
+    1: [([], [[(1, 0)], [(1, 3)]]), (["c3", "s3"], [[(3, 0)], [(3, 1)]]), (["c0", "s0"], [[(0, 1)]]),
+        (["c2", "s2"], [[(2, 1)], [(2, 3)]]), (["fw"], [[(2, 0)]])],
+    2: [(["c1", "s1"], [[(1, 0), (2, 0)], [(2, 1)]]), (["c3", "s3"], [[(3, 0)], [(3, 1)], [(3, 2)]]),
+        (["c0", "s0"], [[(0, 1)]]), (["fw"], [[(0, 2)]])],
+    3: [(["c2", "s2"], [[(2, 1)], [(2, 3)], [(3, 1)], [(3, 2)]]), (["c0", "s0"], [[(0, 2)]]),
+        (["c1", "s1"], [[(1, 3)]]), (["fw"], [[(0, 1)]])]}
+STORES = {
+    0: [(1, (1, 3), (1, 3)), (0, (0, 2), (3, 2)), (1, (1, 0), (2, 0)), (1, (2, 3), (2, 3)), (0, (3, 0), (3, 0))],
+    1: [(0, (1, 0), (1, 0)), (0, (3, 0), (3, 0)), (1, (0, 1), (3, 1)), (1, (1, 3), (2, 3)), (0, (2, 0), (2, 0))],
+    2: [(0, (1, 0), (3, 0)), (0, (3, 2), (3, 2)), (1, (0, 1), (3, 1)), (0, (0, 2), (0, 2))],
+    3: [(0, (2, 1), (3, 1)), (1, (0, 2), (3, 2)), (0, (1, 3), (2, 3)), (0, (0, 1), (0, 1))]}
+
 SCRATCH = {
     "xin": ("sbuf", [128, 512], "bfloat16"),
     "win": ("sbuf", [128, 512], "bfloat16"),
@@ -10,109 +61,58 @@ SCRATCH = {
     "lc": ("sbuf", [128, WIDE], "float8_e4m3fn_x4"),
     "ls": ("sbuf", [128, WIDE], "uint8"),
     "ysb": ("sbuf", [128, 384], "float32"),
-    "ps": ("psum", [128, 2048], "float32"),
+    "ps": ("psum", [128, 2560], "float32"),
 }
-SEMAPHORES = (["xl", "wl", "qx", "qw", "sent", "fw", "st0", "st1"]
-              + ["c%d" % j for j in range(4)] + ["s%d" % j for j in range(4)]
-              + ["mm%d" % k for k in range(4)] + ["cp%d" % k for k in range(6)])
-NC = 128
+LABELS = sorted({tr[3] for calls in CALLS.values() for _, trs in calls for tr in trs})
+SEMAPHORES = (["xl", "wl", "qx", "qw", "sent", "st0", "st1"] + LABELS
+              + ["mm%d" % k for k in range(5)] + ["cp%d" % k for k in range(5)])
 
 
-def _plan(CNT):
-    off = [[sum(c[:e]) for e in range(5)] for c in CNT]
-
-    def run(j, a, b):
-        return off[j][a], off[j][b + 1]
-    al = (0, NC)
-    lay = {0: [(2, al), (3, run(3, 0, 0)), (1, al), (3, run(3, 2, 2))],
-           1: [(2, al), (3, run(3, 0, 1)), (0, al)],
-           2: [(0, al), (1, run(1, 0, 0)), (3, al)],
-           3: [(2, al), (1, run(1, 3, 3)), (0, al)]}
+def _places(CNT):
     place = {}
-    for d in lay:
-        at = NC
-        place[d] = [(d, 0, NC, 0)]
-        for j, (a, b) in lay[d]:
-            place[d].append((j, a, b, at))
-            at += b - a
+    for d, lay in LAY.items():
+        first = [j for j, f0, f1 in lay].index(d)
+        at, place[d] = -sum(CNT[j][f] for j, f0, f1 in lay[:first] for f in range(f0, f1 + 1)) % 16, {}
+        for j, f0, f1 in lay:
+            for f in range(f0, f1 + 1):
+                place[d][j, f] = at
+                at += CNT[j][f]
+    return place
 
-    def col(d, j, c):
-        for jj, a, b, at in place[d]:
-            if jj == j and a <= c < b:
-                return at + c - a
-        raise ValueError("no place")
 
-    def t(kind, span, d):
-        return kind, span[0], span[1], d
-    sends = {
-        0: [[t("c", al, 2)],
-            [t("s", al, 2), t("s", al, 3), t("s", al, 1)],
-            [t("c", run(0, 1, 1), 1)]],
-        1: [[t("c", run(1, 0, 0), 2), t("c", run(1, 0, 0), 0)],
-            [t("c", run(1, 3, 3), 3), t("c", run(1, 3, 3), 0)],
-            [t("s", run(1, 0, 0), 2), t("s", run(1, 0, 0), 0)],
-            [t("s", run(1, 3, 3), 3), t("s", run(1, 3, 3), 0)]],
-        2: [[t("c", al, 1)],
-            [t("s", al, 1), t("s", al, 3)],
-            [t("s", run(2, 0, 0), 0), t("s", run(2, 3, 3), 0)],
-            [t("c", run(2, 1, 3), 3)]],
-        3: [[t("c", run(3, 0, 1), 1)],
-            [t("c", run(3, 2, 2), 0)],
-            [t("s", run(3, 0, 1), 1), t("s", run(3, 0, 1), 2)],
-            [t("s", run(3, 2, 2), 0), t("s", run(3, 2, 2), 2)],
-            [t("s", run(3, 0, 0), 0)],
-            [t("c", al, 2)]]}
-    n0 = run(3, 0, 0)[1] - run(3, 0, 0)[0]
-    passes = {1: (["c2", "c3"], col(1, 2, 0), NC + n0, 0, col(0, 2, 0)),
-              2: (["c0"], col(2, 0, 0), NC, 3, col(3, 0, 0))}
-    q0 = col(0, 2, off[2][3])
-    p1 = col(0, 2, 0) + off[2][1]
-    windows = {
-        0: [(0, NC, [], [(0, 2)]),
-            (col(0, 1, 0), col(0, 3, off[3][2]) + CNT[3][2], ["c1", "s1", "c3", "s3"], [(1, 0), (1, 3), (3, 2)]),
-            (q0, q0 + NC, ["fw", "s2"], [(2, 3), (3, 0)]),
-            (p1 - NC, p1, [], [(2, 0)])],
-        1: [(0, NC, [], [(1, 0), (1, 3)]),
-            (col(1, 2, 0), col(1, 0, 0) + CNT[0][1], ["c0", "s0", "c2", "s2", "c3", "s3"],
-             [(2, 0), (3, 0), (2, 3), (0, 1), (2, 1), (3, 1)])],
-        2: [(0, NC, [], [(2, 1), (2, 0)]),
-            (col(2, 3, 0), col(2, 3, 0) + NC, ["c3", "s3"], [(3, 2), (3, 1), (3, 0)]),
-            (col(2, 0, 0), col(2, 1, 0) + CNT[1][0], ["c0", "s0", "c1", "s1"], [(0, 2), (0, 1), (1, 0)])],
-        3: [(0, NC, [], [(3, 1), (3, 2)]),
-            (col(3, 2, off[2][1]), col(3, 1, off[1][3]) + CNT[1][3], ["c2", "s2", "c1", "s1"], [(2, 1), (2, 3), (1, 3)]),
-            (col(3, 0, 0), col(3, 0, 0) + NC, ["fw", "s0"], [(0, 2), (0, 1)])]}
+def _ycol(CNT, e, j, f):
+    return NC * ((e - f) % 4) + sum(CNT[i][f] for i in range(j))
 
-    def ycol(e, j, f):
-        return NC * ((e - f) % 4) + sum(CNT[i][f] for i in range(j))
 
-    def yspan(e, j, f, j2, f2):
-        return ycol(e, j, f), ycol(e, j2, f2) + CNT[j2][f2]
-    stores = {
-        0: [(0, yspan(0, 1, 0, 1, 0)), (1, yspan(0, 1, 3, 1, 3)), (0, yspan(0, 0, 2, 3, 2)),
-            (1, yspan(0, 2, 3, 2, 3)), (0, yspan(0, 2, 0, 3, 0))],
-        1: [(0, yspan(1, 1, 0, 1, 0)), (1, yspan(1, 1, 3, 1, 3)),
-            (0, yspan(1, 2, 0, 3, 0)), (1, yspan(1, 2, 3, 2, 3)), (0, yspan(1, 0, 1, 3, 1))],
-        2: [(0, yspan(2, 3, 2, 3, 2)), (1, yspan(2, 2, 1, 3, 1)), (0, yspan(2, 2, 0, 3, 0)),
-            (1, yspan(2, 0, 2, 0, 2)), (0, yspan(2, 0, 1, 0, 1)), (1, yspan(2, 1, 0, 1, 0))],
-        3: [(0, yspan(3, 3, 2, 3, 2)), (1, yspan(3, 2, 1, 3, 1)), (0, yspan(3, 1, 3, 2, 3)),
-            (1, yspan(3, 0, 2, 0, 2)), (0, yspan(3, 0, 1, 0, 1))]}
-    return off, col, sends, passes, windows, ycol, stores
+def _window(CNT, place, have, runs):
+    lo = min(place[r] for r in runs)
+    hi = max(place[r] + CNT[r[0]][r[1]] for r in runs)
+    ok = {c for j, f in have for c in range(place[j, f], place[j, f] + CNT[j][f])}
+    assert all(c in ok for c in range(lo, hi))
+    while hi - lo < NC:
+        if lo - 1 in ok:
+            lo -= 1
+        else:
+            assert hi in ok
+            hi += 1
+    return lo, hi
 
 
 def _bits(mask):
     return [1 << k for k in range(mask.bit_length()) if mask >> k & 1]
 
 
-def _masks(call, src, cores, topo):
-    dsts = [cores[tr[3]] for tr in call]
-    away = [topo.host(d) != topo.host(src) or topo.chip(d) != topo.chip(src) for d in dsts]
+def _masks(trs, src, cores, topo):
     far = [c for c in cores if topo.host(c) != topo.host(src)]
+    near = [c for c in cores if c != src and c not in far]
     leave = topo.mask(src, far[0])
+    pools = {"out": leave, "in": topo.mask(src, near[0]) & ~leave, "all": topo.mask(src, near[0])}
     out = []
-    for k, d in enumerate(dsts):
-        pool = _bits(leave if away[k] else topo.mask(src, d) & ~leave)
-        share = len(pool) // away.count(away[k])
-        nth = away[:k].count(away[k])
+    for k, tr in enumerate(trs):
+        pool = _bits(pools[tr[4]])
+        same = [i for i, o in enumerate(trs) if o[4] == tr[4]]
+        share = len(pool) // len(same)
+        nth = same.index(k)
         out.append(sum(pool[nth * share:(nth + 1) * share]))
     return out
 
@@ -123,77 +123,79 @@ def rank_program(g, core, T, topo):
         return
     CNT = T.tables["CNT"]
     cores = T.cores
-    off, col, sends, passes, windows, ycol, stores = _plan(CNT)
-
-    due = {}
-    sent = 0
+    place = _places(CNT)
+    mine = place[me]
+    due, brings, sent = {}, {}, 0
     for r in range(4):
-        for call in sends[r]:
-            for (kind, a, b, d), m in zip(call, _masks(call, cores[r], cores, topo)):
-                if d == me:
-                    due[kind + str(r)] = due.get(kind + str(r), 0) + m.bit_count()
+        for _, trs in CALLS[r]:
+            for tr, m in zip(trs, _masks(trs, cores[r], cores, topo)):
+                if tr[2] == me:
+                    due[tr[3]] = due.get(tr[3], 0) + m.bit_count()
+                    brings.setdefault(tr[3], []).extend((tr[0], run) for run in tr[1])
                 if r == me:
                     sent += m.bit_count()
-        if r in passes:
-            m = topo.mask(cores[r], cores[passes[r][3]])
-            if passes[r][3] == me:
-                due["fw"] = m.bit_count()
-            if r == me:
-                sent += m.bit_count()
+    own = min(at for (j, f), at in mine.items() if j == me)
 
     g.sync.dma_start(T.xin[:], T.x[:]).then_inc(T.sem.xl, 16)
-    g.scalar.wait_ge(T.sem.xl, 16)
-    g.scalar.dma_start(T.win[:], T.w[:]).then_inc(T.sem.wl, 16)
+    g.sync.dma_start(T.win[:], T.w[:]).then_inc(T.sem.wl, 16)
 
     g.vector.wait_ge(T.sem.xl, 16)
-    g.vector.quantize_mx(T.lc[:, 0:NC], T.ls[:, 0:NC], T.xin[:]).then_inc(T.sem.qx, 1)
+    g.vector.quantize_mx(T.lc[:, own:own + NC], T.ls[:, own:own + NC], T.xin[:]).then_inc(T.sem.qx, 1)
     g.vector.wait_ge(T.sem.wl, 16)
     g.vector.quantize_mx(T.wq[:], T.ws[:], T.win[:]).then_inc(T.sem.qw, 1)
 
     def side(kind, a, b):
         return T.lc[:, a:b].bitcast(dt.uint8) if kind == "c" else T.ls[:, a:b]
     g.wait_ge(T.sem.qx, 1)
-    for call in sends[me]:
-        trs = []
-        for (kind, a, b, d), m in zip(call, _masks(call, core, cores, topo)):
+    for waits, trs in CALLS[me]:
+        for s in waits:
+            g.wait_ge(T.sem[s], due[s])
+        todo = []
+        for (kind, runs, d, label, pool), m in zip(trs, _masks(trs, core, cores, topo)):
+            i, o, n = mine[runs[0]], place[d][runs[0]], 0
+            for j, f in runs:
+                assert mine[j, f] == i + n and place[d][j, f] == o + n
+                n += CNT[j][f]
             rid, pid = topo.addr(cores[d], core)
-            at = col(d, me, a)
-            trs.append((side(kind, at, at + b - a), side(kind, a, b), T.sem[kind + str(me)], rid, pid, m))
-        if len(trs) == 1:
-            o, i, s, rid, pid, m = trs[0]
+            todo.append((side(kind, o, o + n), side(kind, i, i + n), T.sem[label], rid, pid, m))
+        if len(todo) == 1:
+            o, i, s, rid, pid, m = todo[0]
             g.remote_dma(out_ap=o, in_ap=i, remote_sem=s, local_sem=T.sem.sent, pid=pid, routing_id=rid, dma_engine_mask=m)
         else:
             g.remote_dma_fused([RemoteDMATransfer(dst_ids=[DstId(rid=rid, pnc=pid)], dma_engine_mask=m, remote_sem=s, src=i, dst=o)
-                                for o, i, s, rid, pid, m in trs], local_sem=T.sem.sent)
-    if me in passes:
-        waits, a, n, d, at = passes[me]
-        for s in waits:
-            g.wait_ge(T.sem[s], due[s])
-        rid, pid = topo.addr(cores[d], core)
-        g.remote_dma(out_ap=side("c", at, at + n), in_ap=side("c", a, a + n), remote_sem=T.sem.fw, local_sem=T.sem.sent,
-                     pid=pid, routing_id=rid, dma_engine_mask=topo.mask(core, cores[d]))
+                                for o, i, s, rid, pid, m in todo], local_sem=T.sem.sent)
     g.wait_ge(T.sem.sent, sent)
 
     g.tensor.wait_ge(T.sem.qx, 1)
     g.tensor.wait_ge(T.sem.qw, 1)
-    for k, (a, b, waits, runs) in enumerate(windows[me]):
+    there = [(kind, (me, f)) for f in range(4) for kind in "cs"]
+    start = []
+    for k, (waits, groups) in enumerate(WINDOWS[me]):
         for s in waits:
             g.tensor.wait_ge(T.sem[s], due[s])
+            there += brings[s]
+        have = [run for kind, run in there if kind == "c" and ("s", run) in there and run in mine]
+        a, b = _window(CNT, mine, have, [r for grp in groups for r in grp])
+        start.append(a)
         g.tensor.matmul_mx(T.ps[:, 512 * k:512 * k + b - a], T.wq[:], T.ws[:], T.lc[:, a:b], T.ls[:, a:b],
                            True, True).then_inc(T.sem["mm%d" % k], 1)
 
-    ready = [0] * len(stores[me])
-    for k, (a, b, waits, runs) in enumerate(windows[me]):
+    stores = [(q, _ycol(CNT, me, *lo), _ycol(CNT, me, *hi) + CNT[hi[0]][hi[1]]) for q, lo, hi in STORES[me]]
+    ready = [0] * len(stores)
+    for k, (waits, groups) in enumerate(WINDOWS[me]):
         g.vector.wait_ge(T.sem["mm%d" % k], 1)
-        for j, f in runs:
-            n, y = CNT[j][f], ycol(me, j, f)
-            p = 512 * k + col(me, j, off[j][f]) - a
-            s = [i for i, (q, (lo, hi)) in enumerate(stores[me]) if lo <= y and y + n <= hi][0]
+        for grp in groups:
+            n, y, p = 0, _ycol(CNT, me, *grp[0]), mine[grp[0]]
+            for j, f in grp:
+                assert mine[j, f] == p + n and _ycol(CNT, me, j, f) == y + n
+                n += CNT[j][f]
+            p += 512 * k - start[k]
+            s = [i for i, (q, lo, hi) in enumerate(stores) if lo <= y and y + n <= hi][0]
             ready[s] += 1
             g.vector.tensor_copy(T.ysb[:, y:y + n], T.ps[:, p:p + n]).then_inc(T.sem["cp%d" % s], 1)
 
     count = [0, 0]
-    for i, (q, (lo, hi)) in enumerate(stores[me]):
+    for i, (q, lo, hi) in enumerate(stores):
         queue = g.scalar if q else g.sync
         queue.wait_ge(T.sem["cp%d" % i], ready[i])
         queue.dma_start(T.y[:, lo:hi], T.ysb[:, lo:hi]).then_inc(T.sem["st%d" % q], 16)

from concourse.bass import DstId, RemoteDMATransfer
from concourse.mybir import dt

NC = 128
WIDE = 512


def _r(j, f0, f1):
    return tuple((j, f) for f in range(f0, f1 + 1))


LAY = {0: [(1, 0, 3), (2, 0, 3), (3, 0, 0), (0, 1, 2), (3, 2, 2)],
       1: [(2, 0, 3), (3, 0, 1), (1, 0, 3), (0, 1, 2)],
       2: [(1, 0, 0), (2, 0, 3), (0, 1, 2), (3, 0, 2)],
       3: [(0, 1, 2), (3, 0, 2), (2, 1, 3), (1, 3, 3)]}
CALLS = {
    0: [([], [("c", _r(0, 2, 2), 3, "c0", "out")]),
        ([], [("c", _r(0, 1, 1), 2, "c0", "out"), ("c", _r(0, 1, 1), 1, "c0", "in")]),
        ([], [("s", _r(0, 1, 2), 2, "s0", "out"), ("s", _r(0, 1, 2), 3, "s0", "out"), ("s", _r(0, 1, 2), 1, "s0", "in")]),
        (["c2"], [("c", _r(2, 0, 0), 1, "fw", "all")])],
    1: [([], [("c", _r(1, 0, 0), 2, "c1", "out")]),
        ([], [("c", _r(1, 0, 3), 0, "c1", "in")]),
        ([], [("c", _r(1, 3, 3), 3, "c1", "out")]),
        ([], [("s", _r(1, 0, 3), 0, "s1", "in")]),
        ([], [("s", _r(1, 0, 0), 2, "s1", "out")]),
        ([], [("s", _r(1, 3, 3), 3, "s1", "out")]),
        (["c2", "c3"], [("c", _r(2, 1, 3) + _r(3, 0, 0), 0, "fw", "all")]),
        (["s3"], [("s", _r(3, 0, 0), 0, "sf", "in")])],
    2: [([], [("c", _r(2, 1, 3), 1, "c2", "out")]),
        ([], [("c", _r(2, 0, 0), 0, "c2", "out")]),
        ([], [("c", _r(2, 1, 3), 3, "c2", "in")]),
        ([], [("s", _r(2, 0, 3), 1, "s2", "out"), ("s", _r(2, 0, 3), 0, "s2", "out")]),
        ([], [("s", _r(2, 1, 3), 3, "s2", "in")]),
        (["c0"], [("c", _r(0, 1, 1), 3, "fw", "all")])],
    3: [([], [("c", _r(3, 0, 1), 1, "c3", "out")]),
        ([], [("s", _r(3, 0, 1), 1, "s3", "out"), ("s", _r(3, 0, 1), 2, "s3", "in")]),
        ([], [("c", _r(3, 2, 2), 0, "c3", "out")]),
        ([], [("c", _r(3, 0, 2), 2, "c3", "in")]),
        ([], [("s", _r(3, 2, 2), 0, "s3", "out"), ("s", _r(3, 2, 2), 2, "s3", "in")]),
        (["c0"], [("c", _r(0, 2, 2), 2, "fw", "all")])]}
WINDOWS = {
    0: [(["c1", "s1"], [[(1, 0)], [(1, 3)]]), (["c3", "s3"], [[(0, 2), (3, 2)]]), (["c2", "s2"], [[(2, 0)]]),
        (["fw"], [[(2, 3)]]), (["sf"], [[(3, 0)]])],
    1: [([], [[(1, 0)], [(1, 3)]]), (["c3", "s3"], [[(3, 0)], [(3, 1)]]), (["c0", "s0"], [[(0, 1)]]),
        (["c2", "s2"], [[(2, 1)], [(2, 3)]]), (["fw"], [[(2, 0)]])],
    2: [(["c1", "s1"], [[(1, 0), (2, 0)], [(2, 1)]]), (["c3", "s3"], [[(3, 0)], [(3, 1)], [(3, 2)]]),
        (["c0", "s0"], [[(0, 1)]]), (["fw"], [[(0, 2)]])],
    3: [(["c2", "s2"], [[(2, 1)], [(2, 3)], [(3, 1)], [(3, 2)]]), (["c0", "s0"], [[(0, 2)]]),
        (["c1", "s1"], [[(1, 3)]]), (["fw"], [[(0, 1)]])]}
STORES = {
    0: [(1, (1, 3), (1, 3)), (0, (0, 2), (3, 2)), (1, (1, 0), (2, 0)), (1, (2, 3), (2, 3)), (0, (3, 0), (3, 0))],
    1: [(0, (1, 0), (1, 0)), (0, (3, 0), (3, 0)), (1, (0, 1), (3, 1)), (1, (1, 3), (2, 3)), (0, (2, 0), (2, 0))],
    2: [(0, (1, 0), (3, 0)), (0, (3, 2), (3, 2)), (1, (0, 1), (3, 1)), (0, (0, 2), (0, 2))],
    3: [(0, (2, 1), (3, 1)), (1, (0, 2), (3, 2)), (0, (1, 3), (2, 3)), (0, (0, 1), (0, 1))]}

SCRATCH = {
    "xin": ("sbuf", [128, 512], "bfloat16"),
    "win": ("sbuf", [128, 512], "bfloat16"),
    "wq": ("sbuf", [128, 128], "float8_e4m3fn_x4"),
    "ws": ("sbuf", [128, 128], "uint8"),
    "lc": ("sbuf", [128, WIDE], "float8_e4m3fn_x4"),
    "ls": ("sbuf", [128, WIDE], "uint8"),
    "ysb": ("sbuf", [128, 384], "float32"),
    "ps": ("psum", [128, 2560], "float32"),
}
LABELS = sorted({tr[3] for calls in CALLS.values() for _, trs in calls for tr in trs})
SEMAPHORES = (["xl", "wl", "qx", "qw", "sent", "st0", "st1"] + LABELS
              + ["mm%d" % k for k in range(5)] + ["cp%d" % k for k in range(5)])


def _places(CNT):
    place = {}
    for d, lay in LAY.items():
        first = [j for j, f0, f1 in lay].index(d)
        at, place[d] = -sum(CNT[j][f] for j, f0, f1 in lay[:first] for f in range(f0, f1 + 1)) % 16, {}
        for j, f0, f1 in lay:
            for f in range(f0, f1 + 1):
                place[d][j, f] = at
                at += CNT[j][f]
    return place


def _ycol(CNT, e, j, f):
    return NC * ((e - f) % 4) + sum(CNT[i][f] for i in range(j))


def _window(CNT, place, have, runs):
    lo = min(place[r] for r in runs)
    hi = max(place[r] + CNT[r[0]][r[1]] for r in runs)
    ok = {c for j, f in have for c in range(place[j, f], place[j, f] + CNT[j][f])}
    assert all(c in ok for c in range(lo, hi))
    while hi - lo < NC:
        if lo - 1 in ok:
            lo -= 1
        else:
            assert hi in ok
            hi += 1
    return lo, hi


def _bits(mask):
    return [1 << k for k in range(mask.bit_length()) if mask >> k & 1]


def _masks(trs, src, cores, topo):
    far = [c for c in cores if topo.host(c) != topo.host(src)]
    near = [c for c in cores if c != src and c not in far]
    leave = topo.mask(src, far[0])
    pools = {"out": leave, "in": topo.mask(src, near[0]) & ~leave, "all": topo.mask(src, near[0])}
    out = []
    for k, tr in enumerate(trs):
        pool = _bits(pools[tr[4]])
        same = [i for i, o in enumerate(trs) if o[4] == tr[4]]
        share = len(pool) // len(same)
        nth = same.index(k)
        out.append(sum(pool[nth * share:(nth + 1) * share]))
    return out


def rank_program(g, core, T, topo):
    me = T.rank_of(core)
    if me is None:
        return
    CNT = T.tables["CNT"]
    cores = T.cores
    place = _places(CNT)
    mine = place[me]
    due, brings, sent = {}, {}, 0
    for r in range(4):
        for _, trs in CALLS[r]:
            for tr, m in zip(trs, _masks(trs, cores[r], cores, topo)):
                if tr[2] == me:
                    due[tr[3]] = due.get(tr[3], 0) + m.bit_count()
                    brings.setdefault(tr[3], []).extend((tr[0], run) for run in tr[1])
                if r == me:
                    sent += m.bit_count()
    own = min(at for (j, f), at in mine.items() if j == me)

    g.sync.dma_start(T.xin[:], T.x[:]).then_inc(T.sem.xl, 16)
    g.sync.dma_start(T.win[:], T.w[:]).then_inc(T.sem.wl, 16)

    g.vector.wait_ge(T.sem.xl, 16)
    g.vector.quantize_mx(T.lc[:, own:own + NC], T.ls[:, own:own + NC], T.xin[:]).then_inc(T.sem.qx, 1)
    g.vector.wait_ge(T.sem.wl, 16)
    g.vector.quantize_mx(T.wq[:], T.ws[:], T.win[:]).then_inc(T.sem.qw, 1)

    def side(kind, a, b):
        return T.lc[:, a:b].bitcast(dt.uint8) if kind == "c" else T.ls[:, a:b]
    g.wait_ge(T.sem.qx, 1)
    for waits, trs in CALLS[me]:
        for s in waits:
            g.wait_ge(T.sem[s], due[s])
        todo = []
        for (kind, runs, d, label, pool), m in zip(trs, _masks(trs, core, cores, topo)):
            i, o, n = mine[runs[0]], place[d][runs[0]], 0
            for j, f in runs:
                assert mine[j, f] == i + n and place[d][j, f] == o + n
                n += CNT[j][f]
            rid, pid = topo.addr(cores[d], core)
            todo.append((side(kind, o, o + n), side(kind, i, i + n), T.sem[label], rid, pid, m))
        if len(todo) == 1:
            o, i, s, rid, pid, m = todo[0]
            g.remote_dma(out_ap=o, in_ap=i, remote_sem=s, local_sem=T.sem.sent, pid=pid, routing_id=rid, dma_engine_mask=m)
        else:
            g.remote_dma_fused([RemoteDMATransfer(dst_ids=[DstId(rid=rid, pnc=pid)], dma_engine_mask=m, remote_sem=s, src=i, dst=o)
                                for o, i, s, rid, pid, m in todo], local_sem=T.sem.sent)
    g.wait_ge(T.sem.sent, sent)

    g.tensor.wait_ge(T.sem.qx, 1)
    g.tensor.wait_ge(T.sem.qw, 1)
    there = [(kind, (me, f)) for f in range(4) for kind in "cs"]
    start = []
    for k, (waits, groups) in enumerate(WINDOWS[me]):
        for s in waits:
            g.tensor.wait_ge(T.sem[s], due[s])
            there += brings[s]
        have = [run for kind, run in there if kind == "c" and ("s", run) in there and run in mine]
        a, b = _window(CNT, mine, have, [r for grp in groups for r in grp])
        start.append(a)
        g.tensor.matmul_mx(T.ps[:, 512 * k:512 * k + b - a], T.wq[:], T.ws[:], T.lc[:, a:b], T.ls[:, a:b],
                           True, True).then_inc(T.sem["mm%d" % k], 1)

    stores = [(q, _ycol(CNT, me, *lo), _ycol(CNT, me, *hi) + CNT[hi[0]][hi[1]]) for q, lo, hi in STORES[me]]
    ready = [0] * len(stores)
    for k, (waits, groups) in enumerate(WINDOWS[me]):
        g.vector.wait_ge(T.sem["mm%d" % k], 1)
        for grp in groups:
            n, y, p = 0, _ycol(CNT, me, *grp[0]), mine[grp[0]]
            for j, f in grp:
                assert mine[j, f] == p + n and _ycol(CNT, me, j, f) == y + n
                n += CNT[j][f]
            p += 512 * k - start[k]
            s = [i for i, (q, lo, hi) in enumerate(stores) if lo <= y and y + n <= hi][0]
            ready[s] += 1
            g.vector.tensor_copy(T.ysb[:, y:y + n], T.ps[:, p:p + n]).then_inc(T.sem["cp%d" % s], 1)

    count = [0, 0]
    for i, (q, lo, hi) in enumerate(stores):
        queue = g.scalar if q else g.sync
        queue.wait_ge(T.sem["cp%d" % i], ready[i])
        queue.dma_start(T.y[:, lo:hi], T.ysb[:, lo:hi]).then_inc(T.sem["st%d" % q], 16)
        count[q] += 16
    g.sync.wait_ge(T.sem.st0, count[0])
    g.scalar.wait_ge(T.sem.st1, count[1])
